import numpy as np
import ml_dtypes


def mxq(x, axis, fmt="e4m3"):
    dtype, down = {"e4m3": (ml_dtypes.float8_e4m3fn, 7), "e5m2": (ml_dtypes.float8_e5m2, 14)}[fmt]
    v = np.moveaxis(np.asarray(x, np.float32).astype(ml_dtypes.bfloat16).astype(np.float64), axis, -1)
    blocks = v.reshape(v.shape[:-1] + (-1, 32))
    amax = np.abs(blocks).max(-1, keepdims=True)
    byte = np.maximum(np.where(amax > 0, np.frexp(amax)[1] - 1 + 127, 0) - down, 1)
    scale = np.exp2(byte - 127.0)
    codes = (blocks / scale).astype(np.float32).astype(dtype).astype(np.float64)
    return np.moveaxis((codes * scale).reshape(v.shape), -1, axis)


WIDE = False


def mx_kscale(k):
    if not WIDE:
        return np.ones(k)
    levels = np.array([10, -10, 5, -5, 0])
    if k % 512:
        return np.exp2(np.random.permutation(np.resize(levels, k // 32))).repeat(32)
    a = np.empty((k // 512, 16))
    for p in range(k // 512):
        a[p, :8] = np.random.permutation(np.resize(levels, 8))
        for g in range(8):
            far = levels[np.abs(levels - a[p, g]) >= 10]
            a[p, g + 8] = far[np.random.randint(len(far))]
    return np.exp2(a.ravel()).repeat(32)


def f64(x):
    return np.asarray(x).astype(np.float64)


def striped8(idx):
    return np.concatenate([v.reshape(-1, 16).T for v in idx]).astype(np.uint16)


def unstriped8(offs):
    return np.stack([offs[16 * g:16 * g + 16].T.reshape(-1) for g in range(8)]).astype(np.int64)


E2M1 = np.array([0.0, 0.5, 1.0, 1.5, 2.0, 3.0, 4.0, 6.0, -0.0, -0.5, -1.0, -1.5, -2.0, -3.0, -4.0, -6.0])


def pack_weight(w, fmt):
    k, n = w.shape
    w = f64(np.asarray(w, np.float32).astype(ml_dtypes.bfloat16)).reshape(k // 32, 32, n)
    amax = np.abs(w).max(1)
    if fmt == "e4m3":
        byte = np.frexp(amax)[1] - 1 + 127 - 7
    else:
        mant, ex = np.frexp(amax / 6.0)
        byte = np.where(mant > 0.5, ex, ex - 1) + 127
    byte = np.clip(np.where(amax > 0, byte, 1), 1, 254)
    scaled = (w * np.exp2(127.0 - byte)[:, None, :]).reshape(k, n).astype(np.float32)
    by_word = np.ascontiguousarray(scaled.reshape(k // 512, 128, 4, n).transpose(0, 1, 3, 2))
    if fmt == "e4m3":
        words = by_word.astype(ml_dtypes.float8_e4m3fn).view(np.uint8)
    else:
        c = by_word.astype(ml_dtypes.float4_e2m1fn).view(np.uint8) & 0xF
        words = (c[..., 0::2] | (c[..., 1::2] << 4)).reshape(k // 512, 128, 2 * n)
    return np.ascontiguousarray(words), np.ascontiguousarray(byte.astype(np.uint8).reshape(k // 512, 16, n))


def unpack_weight(words, scales, fmt):
    g, _, n = scales.shape
    words = np.ascontiguousarray(words).reshape(g, 128, n, -1)
    if fmt == "e4m3":
        vals = words.view(ml_dtypes.float8_e4m3fn).astype(np.float64)
    else:
        nib = np.empty((g, 128, n, 4), np.uint8)
        nib[..., 0::2] = words & 0xF
        nib[..., 1::2] = words >> 4
        vals = E2M1[nib]
    vals = vals * np.repeat(np.exp2(scales.astype(np.float64) - 127.0), 8, axis=1)[..., None]
    return vals.transpose(0, 1, 3, 2).reshape(g * 512, n)


K, M, T, S = 1024, 1024, 1024, 512


def setup_inputs():
    n = np.random.standard_normal
    s = mx_kscale(K)[:, None]
    w = n((K, M)) / np.sqrt(K) / s
    p_w8 = pack_weight(w[:512], "e4m3")
    p_w4 = pack_weight(w[512:], "e2m1")
    return {
        "x": (n((K, S)) * s).astype(np.float32),
        "w8_words": p_w8[0],
        "w8_scales": p_w8[1],
        "w4_words": p_w4[0],
        "w4_scales": p_w4[1],
        "b": (0.3 * n(1024)).astype(np.float32),
        "wgo": np.repeat(np.random.uniform(0.5, 2.0, (8, S)), 16, axis=0).astype(np.float32),
        "offs": striped8(np.stack([np.random.permutation(T)[:S] for _ in range(8)])),
    }


def reference(x, w8_words, w8_scales, w4_words, w4_scales, b, wgo, offs):
    x_ = mxq(f64(x), 0, "e4m3")
    w8_ = unpack_weight(w8_words, w8_scales, "e4m3")
    w4_ = unpack_weight(w4_words, w4_scales, "e2m1")
    y = w8_.T @ x_[:512] + w4_.T @ x_[512:]
    place = unstriped8(offs)[np.arange(M) % 128 // 16]
    out = np.zeros((M, T))
    out[np.arange(M)[:, None], place] = f64(wgo)[np.arange(M) % 128] * (y + f64(b)[:, None])
    return out

@@ -1,0 +1,167 @@
+from contextlib import ExitStack
+
+import concourse.mybir as mybir
+
+K, M, T, S = 1024, 1024, 1024, 512
+FLOPS = 2 * K * M * S
+
+F32 = mybir.dt.float32
+BF16 = mybir.dt.bfloat16
+I32 = mybir.dt.int32
+U32 = mybir.dt.uint32
+U16 = mybir.dt.uint16
+U8 = mybir.dt.uint8
+FP8X4 = mybir.dt.float8_e4m3fn_x4
+FP4X4 = mybir.dt.float4_e2m1fn_x4
+MULT = mybir.AluOpType.mult
+IDENTITY = mybir.ActivationFunctionType.Identity
+
+P = 128
+PACK = 4
+K_PASS = P * PACK
+ROW_TILES = M // P
+PAGES = 4
+CHUNKS = ((0, 128), (128, 256), (256, 512))
+N_SMALL = 128
+
+
+def tile_list_hscat_o_bias_kernel(
+    tc, x, w8_words, w8_scales, w4_words, w4_scales, b, wgo, offs, out
+):
+    nc = tc.nc
+    with ExitStack() as ctx:
+        keep = ctx.enter_context(tc.tile_pool(name="keep", bufs=1))
+        ring = ctx.enter_context(tc.tile_pool(name="ring", bufs=4))
+        psum = ctx.enter_context(tc.psum_pool(name="psum", bufs=8))
+
+        offsets = keep.tile([P, S // 16], U16, name="offsets")
+        w_scale = [keep.tile([P, M], U8, name="w_scale_%d" % a, align_bytes=64) for a in range(2)]
+        half = M // 2
+        w8 = [keep.tile([P, half], I32, name="w8_%d" % h, align_bytes=64) for h in range(2)]
+        w4 = [keep.tile([P, half // 2], I32, name="w4_%d" % h, align_bytes=64) for h in range(2)]
+        gate = keep.tile([P, S], F32, name="gate")
+        raw = [
+            [keep.tile([P, PACK, c1 - c0], F32, name="raw_%d_%d" % (c0, a), tag="raw_%d_%d" % (c0, a)) for a in range(2)]
+            for c0, c1 in CHUNKS
+        ]
+        grouped = [
+            [keep.tile([P, c1 - c0, PACK], BF16, name="grouped_%d_%d" % (c0, a), align_bytes=64) for a in range(2)]
+            for c0, c1 in CHUNKS
+        ]
+        x_codes = [keep.tile([P, S], U32, name="x_codes_%d" % a, align_bytes=64) for a in range(2)]
+        x_scale = [keep.tile([P, S], U8, name="x_scale_%d" % a, align_bytes=64) for a in range(2)]
+        pages = [keep.tile([P, T], F32, name="page_%d" % g) for g in range(PAGES)]
+        b_rows = keep.tile([P, 32], F32, name="b_rows", align_bytes=64)
+        b_cols = keep.tile([P, 32], F32, name="b_cols", align_bytes=64)
+
+        w8_dram = w8_words[0].rearrange("p n t -> p (n t)").bitcast(I32)
+        w4_dram = w4_words[0].bitcast(I32)
+
+        def load_x(queue, c, a):
+            c0, c1 = CHUNKS[c]
+            rows = x[a * K_PASS : (a + 1) * K_PASS, c0:c1]
+            queue.dma_start(out=raw[c][a][:], in_=rows.rearrange("(p i) j -> p i j", i=PACK))
+
+        def load_scales(a, scales, queues):
+            for q in range(4):
+                queues[q % len(queues)].dma_start(
+                    out=w_scale[a][32 * q : 32 * q + 4, :].bitcast(I32),
+                    in_=scales[0, 4 * q : 4 * q + 4, :].bitcast(I32),
+                )
+
+        def load_w8(h):
+            nc.sync.dma_start(out=w8[h][:], in_=w8_dram[:, h * half : (h + 1) * half])
+
+        def load_w4(queue, h):
+            queue.dma_start(out=w4[h][:], in_=w4_dram[:, h * half // 2 : (h + 1) * half // 2])
+
+        def interleave(copy, c, a):
+            copy(
+                out=grouped[c][a][:].rearrange("p (j u) i -> p j i u", u=4),
+                in_=raw[c][a][:].rearrange("p i (j u) -> p j i u", u=4),
+            )
+
+        def quantize(c, a):
+            c0, c1 = CHUNKS[c]
+            nc.vector.quantize_mx(
+                out=x_codes[a][:, c0:c1].bitcast(FP8X4),
+                scales=x_scale[a][:, c0:c1],
+                in_=grouped[c][a][:].rearrange("p j i -> p (j i)"),
+            )
+
+        def place(m, c0, c1, after=None):
+            h, r = divmod(m, ROW_TILES // 2)
+            acc = psum.tile([P, c1 - c0], F32, name="acc")
+            step = S if c1 - c0 == S else N_SMALL
+            for n0 in range(c0, c1, step):
+                cols = slice(n0, n0 + step)
+                dst = acc[:, n0 - c0 : n0 - c0 + step]
+                nc.tensor.matmul_mx(
+                    out=dst,
+                    lhsT=w8[h][:, r * P : (r + 1) * P].bitcast(FP8X4),
+                    lhsT_scale=w_scale[0][:, m * P : (m + 1) * P],
+                    rhs=x_codes[0][:, cols].bitcast(FP8X4),
+                    rhs_scale=x_scale[0][:, cols],
+                    start=True,
+                    stop=False,
+                )
+                nc.tensor.matmul_mx(
+                    out=dst,
+                    lhsT=w4[h][:, r * P // 2 : (r + 1) * P // 2].bitcast(U8).bitcast(FP4X4),
+                    lhsT_scale=w_scale[1][:, m * P : (m + 1) * P],
+                    rhs=x_codes[1][:, cols].bitcast(FP8X4),
+                    rhs_scale=x_scale[1][:, cols],
+                    start=False,
+                    stop=True,
+                )
+            if after is None:
+                y = ring.tile([P, c1 - c0], F32, name="y")
+            else:
+                y = keep.tile([P, c1 - c0], F32, name="y_late_%d" % c0, tag=after)
+            nc.scalar.activation(out=y[:], in_=acc[:], func=IDENTITY, bias=b_cols[:, 4 * m : 4 * m + 1])
+            page = pages[m % PAGES]
+            nc.vector.tensor_tensor(
+                page[:].indirect(offsets[:, c0 // 16 : c1 // 16]), y[:], gate[:, c0:c1], MULT
+            )
+            if c1 == S:
+                nc.sync.dma_start(out=out[m * P : (m + 1) * P, :], in_=page[:])
+
+        for plane in w_scale:
+            nc.vector.memset(plane[:].bitcast(I32), 0)
+        nc.vector.memset(b_rows[:], 0.0)
+
+        first = CHUNKS[0][1]
+        nc.sync.dma_start(offsets[:], offs)
+        load_w4(nc.scalar, 0)
+        load_scales(0, w8_scales, (nc.sync, nc.scalar))
+        load_x(nc.sync, 0, 0)
+        load_x(nc.scalar, 0, 1)
+        load_w8(0)
+        nc.sync.dma_start(out=b_rows[0:P:4, :], in_=b.rearrange("(m q i) -> q m i", q=4, i=32))
+        load_scales(1, w4_scales, (nc.sync,))
+        nc.sync.dma_start(out=gate[:, 0:first], in_=wgo[:, 0:first])
+        load_x(nc.sync, 1, 0)
+        load_x(nc.sync, 1, 1)
+        nc.sync.dma_start(out=gate[:, first:S], in_=wgo[:, first:S])
+        load_x(nc.sync, 2, 0)
+        load_x(nc.sync, 2, 1)
+        load_w8(1)
+        load_w4(nc.sync, 1)
+
+        for page in pages:
+            nc.vector.memset(page[:], 0.0)
+
+        nc.vector.transpose(b_cols[:], b_rows[:])
+
+        for c, (c0, c1) in enumerate(CHUNKS):
+            interleave(nc.scalar.copy, c, 0)
+            interleave(nc.vector.tensor_copy if c == 0 else nc.scalar.copy, c, 1)
+            quantize(c, 0)
+            quantize(c, 1)
+            if c > 0:
+                place(PAGES - 1, *CHUNKS[c - 1], after="raw_%d_1" % c0)
+            for m in range(PAGES - 1):
+                place(m, c0, c1)
+        place(PAGES - 1, *CHUNKS[-1])
+        for m in range(PAGES, ROW_TILES):
+            place(m, 0, S)

@@ -20,9 +20,15 @@ P = 128
 PACK = 4
 K_PASS = P * PACK
 ROW_TILES = M // P
-PAGES = 4
-CHUNKS = ((0, 128), (128, 256), (256, 512))
-N_SMALL = 128
+PAGES = 6
+HELD = 3
+EARLY = PAGES - HELD
+CHUNK = 128
+CHUNKS = tuple(slice(c0, c0 + CHUNK) for c0 in range(0, S, CHUNK))
+
+
+def width(cols):
+    return cols.stop - cols.start
 
 
 def tile_list_hscat_o_bias_kernel(
@@ -31,26 +37,26 @@ def tile_list_hscat_o_bias_kernel(
     nc = tc.nc
     with ExitStack() as ctx:
         keep = ctx.enter_context(tc.tile_pool(name="keep", bufs=1))
-        ring = ctx.enter_context(tc.tile_pool(name="ring", bufs=4))
-        psum = ctx.enter_context(tc.psum_pool(name="psum", bufs=8))
+        psum = ctx.enter_context(tc.psum_pool(name="psum", bufs=1))
 
         offsets = keep.tile([P, S // 16], U16, name="offsets")
         w_scale = [keep.tile([P, M], U8, name="w_scale_%d" % a, align_bytes=64) for a in range(2)]
-        half = M // 2
-        w8 = [keep.tile([P, half], I32, name="w8_%d" % h, align_bytes=64) for h in range(2)]
-        w4 = [keep.tile([P, half // 2], I32, name="w4_%d" % h, align_bytes=64) for h in range(2)]
+        parts = ((0, EARLY), (EARLY, PAGES), (PAGES, ROW_TILES))
+        w8 = [keep.tile([P, (m1 - m0) * P], I32, name="w8_%d" % m0, align_bytes=64) for m0, m1 in parts]
+        w4 = [keep.tile([P, (m1 - m0) * P // 2], I32, name="w4_%d" % m0, align_bytes=64) for m0, m1 in parts]
         gate = keep.tile([P, S], F32, name="gate")
         raw = [
-            [keep.tile([P, PACK, c1 - c0], F32, name="raw_%d_%d" % (c0, a), tag="raw_%d_%d" % (c0, a)) for a in range(2)]
-            for c0, c1 in CHUNKS
+            [
+                keep.tile([P, PACK, width(cols)], F32, name="raw_%d_%d" % (c, a), tag="raw_%d_%d" % (c, a))
+                for a in range(2)
+            ]
+            for c, cols in enumerate(CHUNKS)
         ]
-        grouped = [
-            [keep.tile([P, c1 - c0, PACK], BF16, name="grouped_%d_%d" % (c0, a), align_bytes=64) for a in range(2)]
-            for c0, c1 in CHUNKS
-        ]
-        x_codes = [keep.tile([P, S], U32, name="x_codes_%d" % a, align_bytes=64) for a in range(2)]
-        x_scale = [keep.tile([P, S], U8, name="x_scale_%d" % a, align_bytes=64) for a in range(2)]
-        pages = [keep.tile([P, T], F32, name="page_%d" % g) for g in range(PAGES)]
+        x_codes = [keep.tile([P, 2 * CHUNK], U32, name="x_codes_%d" % c, align_bytes=64) for c in range(len(CHUNKS))]
+        x_scale = [keep.tile([P, 2 * CHUNK], U8, name="x_scale_%d" % c, align_bytes=64) for c in range(len(CHUNKS))]
+        pages = [keep.tile([P, T], F32, name="page_%d" % g) for g in range(PAGES - 1)]
+        accs = [psum.tile([P, S], F32, name="acc_%d" % m) for m in range(ROW_TILES)]
+        ys = [keep.tile([P, S], F32, name="y_%d" % m) for m in range(ROW_TILES)]
         b_rows = keep.tile([P, 32], F32, name="b_rows", align_bytes=64)
         b_cols = keep.tile([P, 32], F32, name="b_cols", align_bytes=64)
 
@@ -58,8 +64,7 @@ def tile_list_hscat_o_bias_kernel(
         w4_dram = w4_words[0].bitcast(I32)
 
         def load_x(queue, c, a):
-            c0, c1 = CHUNKS[c]
-            rows = x[a * K_PASS : (a + 1) * K_PASS, c0:c1]
+            rows = x[a * K_PASS : (a + 1) * K_PASS, CHUNKS[c]]
             queue.dma_start(out=raw[c][a][:], in_=rows.rearrange("(p i) j -> p i j", i=PACK))
 
         def load_scales(a, scales, queues):
@@ -70,98 +75,101 @@ def tile_list_hscat_o_bias_kernel(
                 )
 
         def load_w8(h):
-            nc.sync.dma_start(out=w8[h][:], in_=w8_dram[:, h * half : (h + 1) * half])
+            m0, m1 = parts[h]
+            nc.sync.dma_start(out=w8[h][:], in_=w8_dram[:, m0 * P : m1 * P])
 
         def load_w4(queue, h):
-            queue.dma_start(out=w4[h][:], in_=w4_dram[:, h * half // 2 : (h + 1) * half // 2])
+            m0, m1 = parts[h]
+            queue.dma_start(out=w4[h][:], in_=w4_dram[:, m0 * P // 2 : m1 * P // 2])
 
-        def interleave(copy, c, a):
-            copy(
-                out=grouped[c][a][:].rearrange("p (j u) i -> p j i u", u=4),
-                in_=raw[c][a][:].rearrange("p i (j u) -> p j i u", u=4),
-            )
-
-        def quantize(c, a):
-            c0, c1 = CHUNKS[c]
-            nc.vector.quantize_mx(
-                out=x_codes[a][:, c0:c1].bitcast(FP8X4),
-                scales=x_scale[a][:, c0:c1],
-                in_=grouped[c][a][:].rearrange("p j i -> p (j i)"),
-            )
-
-        def place(m, c0, c1, after=None):
-            h, r = divmod(m, ROW_TILES // 2)
-            acc = psum.tile([P, c1 - c0], F32, name="acc")
-            step = S if c1 - c0 == S else N_SMALL
-            for n0 in range(c0, c1, step):
-                cols = slice(n0, n0 + step)
-                dst = acc[:, n0 - c0 : n0 - c0 + step]
-                nc.tensor.matmul_mx(
-                    out=dst,
-                    lhsT=w8[h][:, r * P : (r + 1) * P].bitcast(FP8X4),
-                    lhsT_scale=w_scale[0][:, m * P : (m + 1) * P],
-                    rhs=x_codes[0][:, cols].bitcast(FP8X4),
-                    rhs_scale=x_scale[0][:, cols],
-                    start=True,
-                    stop=False,
+        def quantize_chunk(c):
+            name = "grouped_%d" % c
+            grouped = keep.tile([P, 2, CHUNK, PACK], BF16, name=name, tag=name, align_bytes=64)
+            for a in range(2):
+                copy = nc.vector.tensor_copy if (c, a) == (0, 1) else nc.scalar.copy
+                copy(
+                    out=grouped[:, a].rearrange("p (j u) i -> p j i u", u=4),
+                    in_=raw[c][a][:].rearrange("p i (j u) -> p j i u", u=4),
                 )
-                nc.tensor.matmul_mx(
-                    out=dst,
-                    lhsT=w4[h][:, r * P // 2 : (r + 1) * P // 2].bitcast(U8).bitcast(FP4X4),
-                    lhsT_scale=w_scale[1][:, m * P : (m + 1) * P],
-                    rhs=x_codes[1][:, cols].bitcast(FP8X4),
-                    rhs_scale=x_scale[1][:, cols],
-                    start=False,
-                    stop=True,
+            halves = (slice(0, 1), slice(1, 2)) if c == 0 else (slice(0, 2),)
+            for h in halves:
+                words = slice(h.start * CHUNK, h.stop * CHUNK)
+                nc.vector.quantize_mx(
+                    out=x_codes[c][:, words].bitcast(FP8X4),
+                    scales=x_scale[c][:, words],
+                    in_=grouped[:, h].rearrange("p a j i -> p (a j i)"),
                 )
-            if after is None:
-                y = ring.tile([P, c1 - c0], F32, name="y")
-            else:
-                y = keep.tile([P, c1 - c0], F32, name="y_late_%d" % c0, tag=after)
-            nc.scalar.activation(out=y[:], in_=acc[:], func=IDENTITY, bias=b_cols[:, 4 * m : 4 * m + 1])
+
+        def place(m, cols, y):
+            h = m // EARLY
+            r = m - parts[h][0]
+            for c in range(cols.start // CHUNK, cols.stop // CHUNK):
+                part = CHUNKS[c]
+                passes = [
+                    (w4[h][:, r * P // 2 : (r + 1) * P // 2].bitcast(U8).bitcast(FP4X4), 1),
+                    (w8[h][:, r * P : (r + 1) * P].bitcast(FP8X4), 0),
+                ]
+                for i, (weights, a) in enumerate(reversed(passes) if (m, c) == (0, 0) else passes):
+                    words = slice(a * CHUNK, (a + 1) * CHUNK)
+                    nc.tensor.matmul_mx(
+                        out=accs[m][:, part],
+                        lhsT=weights,
+                        lhsT_scale=w_scale[a][:, m * P : (m + 1) * P],
+                        rhs=x_codes[c][:, words].bitcast(FP8X4),
+                        rhs_scale=x_scale[c][:, words],
+                        start=(i == 0),
+                        stop=(i == 1),
+                    )
+            nc.scalar.activation(out=y, in_=accs[m][:, cols], func=IDENTITY, bias=b_cols[:, 4 * m : 4 * m + 1])
             page = pages[m % PAGES]
+            c0, c1 = cols.start, cols.stop
             nc.vector.tensor_tensor(
-                page[:].indirect(offsets[:, c0 // 16 : c1 // 16]), y[:], gate[:, c0:c1], MULT
+                page[:].indirect(offsets[:, c0 // 16 : c1 // 16]), y, gate[:, cols], MULT
             )
             if c1 == S:
                 nc.sync.dma_start(out=out[m * P : (m + 1) * P, :], in_=page[:])
 
-        for plane in w_scale:
-            nc.vector.memset(plane[:].bitcast(I32), 0)
         nc.vector.memset(b_rows[:], 0.0)
 
-        first = CHUNKS[0][1]
         nc.sync.dma_start(offsets[:], offs)
+        load_scales(0, w8_scales, (nc.scalar, nc.sync))
+        load_x(nc.scalar, 0, 0)
+        load_x(nc.sync, 0, 1)
         load_w4(nc.scalar, 0)
-        load_scales(0, w8_scales, (nc.sync, nc.scalar))
-        load_x(nc.sync, 0, 0)
-        load_x(nc.scalar, 0, 1)
         load_w8(0)
-        nc.sync.dma_start(out=b_rows[0:P:4, :], in_=b.rearrange("(m q i) -> q m i", q=4, i=32))
         load_scales(1, w4_scales, (nc.sync,))
-        nc.sync.dma_start(out=gate[:, 0:first], in_=wgo[:, 0:first])
+        nc.sync.dma_start(out=b_rows[0:P:4, :], in_=b.rearrange("(m q i) -> q m i", q=4, i=32))
+        nc.sync.dma_start(out=gate[:, CHUNKS[0]], in_=wgo[:, CHUNKS[0]])
         load_x(nc.sync, 1, 0)
-        load_x(nc.sync, 1, 1)
-        nc.sync.dma_start(out=gate[:, first:S], in_=wgo[:, first:S])
-        load_x(nc.sync, 2, 0)
-        load_x(nc.sync, 2, 1)
-        load_w8(1)
         load_w4(nc.sync, 1)
+        load_w8(1)
+        load_x(nc.sync, 1, 1)
+        nc.sync.dma_start(out=gate[:, CHUNKS[0].stop : S], in_=wgo[:, CHUNKS[0].stop : S])
+        for c in range(2, len(CHUNKS)):
+            load_x(nc.sync, c, 0)
+            load_x(nc.sync, c, 1)
+        load_w4(nc.sync, 2)
+        load_w8(2)
 
-        for page in pages:
-            nc.vector.memset(page[:], 0.0)
+        for page in pages[:-1]:
+            nc.vector.memset(page[:].bitcast(I32), 0)
+        nc.gpsimd.memset(pages[-1][:].bitcast(I32), 0)
 
-        nc.vector.transpose(b_cols[:], b_rows[:])
-
-        for c, (c0, c1) in enumerate(CHUNKS):
-            interleave(nc.scalar.copy, c, 0)
-            interleave(nc.vector.tensor_copy if c == 0 else nc.scalar.copy, c, 1)
-            quantize(c, 0)
-            quantize(c, 1)
-            if c > 0:
-                place(PAGES - 1, *CHUNKS[c - 1], after="raw_%d_1" % c0)
-            for m in range(PAGES - 1):
-                place(m, c0, c1)
-        place(PAGES - 1, *CHUNKS[-1])
+        for c, cols in enumerate(CHUNKS):
+            quantize_chunk(c)
+            if c == 0:
+                nc.vector.transpose(b_cols[:], b_rows[:])
+                last_page = keep.tile([P, T], F32, name="last_page", tag="grouped_0", align_bytes=64)
+                nc.vector.memset(last_page[:].bitcast(I32), 0)
+                pages.append(last_page)
+            else:
+                before = CHUNKS[c - 1]
+                y_held = keep.tile([P, HELD, width(before)], F32, name="y_held_%d" % c, tag="raw_%d_1" % c)
+                for m in range(EARLY, PAGES):
+                    place(m, before, y_held[:, m - EARLY])
+            for m in range(EARLY):
+                place(m, cols, ys[m][:, cols])
+        for m in range(EARLY, PAGES):
+            place(m, CHUNKS[-1], ys[m][:, CHUNKS[-1]])
         for m in range(PAGES, ROW_TILES):
-            place(m, 0, S)
+            place(m, slice(0, S), ys[m][:])

from contextlib import ExitStack

import concourse.mybir as mybir

K, M, T, S = 1024, 1024, 1024, 512
FLOPS = 2 * K * M * S

F32 = mybir.dt.float32
BF16 = mybir.dt.bfloat16
I32 = mybir.dt.int32
U32 = mybir.dt.uint32
U16 = mybir.dt.uint16
U8 = mybir.dt.uint8
FP8X4 = mybir.dt.float8_e4m3fn_x4
FP4X4 = mybir.dt.float4_e2m1fn_x4
MULT = mybir.AluOpType.mult
IDENTITY = mybir.ActivationFunctionType.Identity

P = 128
PACK = 4
K_PASS = P * PACK
ROW_TILES = M // P
PAGES = 6
HELD = 3
EARLY = PAGES - HELD
CHUNK = 128
CHUNKS = tuple(slice(c0, c0 + CHUNK) for c0 in range(0, S, CHUNK))


def width(cols):
    return cols.stop - cols.start


def tile_list_hscat_o_bias_kernel(
    tc, x, w8_words, w8_scales, w4_words, w4_scales, b, wgo, offs, out
):
    nc = tc.nc
    with ExitStack() as ctx:
        keep = ctx.enter_context(tc.tile_pool(name="keep", bufs=1))
        psum = ctx.enter_context(tc.psum_pool(name="psum", bufs=1))

        offsets = keep.tile([P, S // 16], U16, name="offsets")
        w_scale = [keep.tile([P, M], U8, name="w_scale_%d" % a, align_bytes=64) for a in range(2)]
        parts = ((0, EARLY), (EARLY, PAGES), (PAGES, ROW_TILES))
        w8 = [keep.tile([P, (m1 - m0) * P], I32, name="w8_%d" % m0, align_bytes=64) for m0, m1 in parts]
        w4 = [keep.tile([P, (m1 - m0) * P // 2], I32, name="w4_%d" % m0, align_bytes=64) for m0, m1 in parts]
        gate = keep.tile([P, S], F32, name="gate")
        raw = [
            [
                keep.tile([P, PACK, width(cols)], F32, name="raw_%d_%d" % (c, a), tag="raw_%d_%d" % (c, a))
                for a in range(2)
            ]
            for c, cols in enumerate(CHUNKS)
        ]
        x_codes = [keep.tile([P, 2 * CHUNK], U32, name="x_codes_%d" % c, align_bytes=64) for c in range(len(CHUNKS))]
        x_scale = [keep.tile([P, 2 * CHUNK], U8, name="x_scale_%d" % c, align_bytes=64) for c in range(len(CHUNKS))]
        pages = [keep.tile([P, T], F32, name="page_%d" % g) for g in range(PAGES - 1)]
        accs = [psum.tile([P, S], F32, name="acc_%d" % m) for m in range(ROW_TILES)]
        ys = [keep.tile([P, S], F32, name="y_%d" % m) for m in range(ROW_TILES)]
        b_rows = keep.tile([P, 32], F32, name="b_rows", align_bytes=64)
        b_cols = keep.tile([P, 32], F32, name="b_cols", align_bytes=64)

        w8_dram = w8_words[0].rearrange("p n t -> p (n t)").bitcast(I32)
        w4_dram = w4_words[0].bitcast(I32)

        def load_x(queue, c, a):
            rows = x[a * K_PASS : (a + 1) * K_PASS, CHUNKS[c]]
            queue.dma_start(out=raw[c][a][:], in_=rows.rearrange("(p i) j -> p i j", i=PACK))

        def load_scales(a, scales, queues):
            for q in range(4):
                queues[q % len(queues)].dma_start(
                    out=w_scale[a][32 * q : 32 * q + 4, :].bitcast(I32),
                    in_=scales[0, 4 * q : 4 * q + 4, :].bitcast(I32),
                )

        def load_w8(h):
            m0, m1 = parts[h]
            nc.sync.dma_start(out=w8[h][:], in_=w8_dram[:, m0 * P : m1 * P])

        def load_w4(queue, h):
            m0, m1 = parts[h]
            queue.dma_start(out=w4[h][:], in_=w4_dram[:, m0 * P // 2 : m1 * P // 2])

        def quantize_chunk(c):
            name = "grouped_%d" % c
            grouped = keep.tile([P, 2, CHUNK, PACK], BF16, name=name, tag=name, align_bytes=64)
            for a in range(2):
                copy = nc.vector.tensor_copy if (c, a) == (0, 1) else nc.scalar.copy
                copy(
                    out=grouped[:, a].rearrange("p (j u) i -> p j i u", u=4),
                    in_=raw[c][a][:].rearrange("p i (j u) -> p j i u", u=4),
                )
            halves = (slice(0, 1), slice(1, 2)) if c == 0 else (slice(0, 2),)
            for h in halves:
                words = slice(h.start * CHUNK, h.stop * CHUNK)
                nc.vector.quantize_mx(
                    out=x_codes[c][:, words].bitcast(FP8X4),
                    scales=x_scale[c][:, words],
                    in_=grouped[:, h].rearrange("p a j i -> p (a j i)"),
                )

        def place(m, cols, y):
            h = m // EARLY
            r = m - parts[h][0]
            for c in range(cols.start // CHUNK, cols.stop // CHUNK):
                part = CHUNKS[c]
                passes = [
                    (w4[h][:, r * P // 2 : (r + 1) * P // 2].bitcast(U8).bitcast(FP4X4), 1),
                    (w8[h][:, r * P : (r + 1) * P].bitcast(FP8X4), 0),
                ]
                for i, (weights, a) in enumerate(reversed(passes) if (m, c) == (0, 0) else passes):
                    words = slice(a * CHUNK, (a + 1) * CHUNK)
                    nc.tensor.matmul_mx(
                        out=accs[m][:, part],
                        lhsT=weights,
                        lhsT_scale=w_scale[a][:, m * P : (m + 1) * P],
                        rhs=x_codes[c][:, words].bitcast(FP8X4),
                        rhs_scale=x_scale[c][:, words],
                        start=(i == 0),
                        stop=(i == 1),
                    )
            nc.scalar.activation(out=y, in_=accs[m][:, cols], func=IDENTITY, bias=b_cols[:, 4 * m : 4 * m + 1])
            page = pages[m % PAGES]
            c0, c1 = cols.start, cols.stop
            nc.vector.tensor_tensor(
                page[:].indirect(offsets[:, c0 // 16 : c1 // 16]), y, gate[:, cols], MULT
            )
            if c1 == S:
                nc.sync.dma_start(out=out[m * P : (m + 1) * P, :], in_=page[:])

        nc.vector.memset(b_rows[:], 0.0)

        nc.sync.dma_start(offsets[:], offs)
        load_scales(0, w8_scales, (nc.scalar, nc.sync))
        load_x(nc.scalar, 0, 0)
        load_x(nc.sync, 0, 1)
        load_w4(nc.scalar, 0)
        load_w8(0)
        load_scales(1, w4_scales, (nc.sync,))
        nc.sync.dma_start(out=b_rows[0:P:4, :], in_=b.rearrange("(m q i) -> q m i", q=4, i=32))
        nc.sync.dma_start(out=gate[:, CHUNKS[0]], in_=wgo[:, CHUNKS[0]])
        load_x(nc.sync, 1, 0)
        load_w4(nc.sync, 1)
        load_w8(1)
        load_x(nc.sync, 1, 1)
        nc.sync.dma_start(out=gate[:, CHUNKS[0].stop : S], in_=wgo[:, CHUNKS[0].stop : S])
        for c in range(2, len(CHUNKS)):
            load_x(nc.sync, c, 0)
            load_x(nc.sync, c, 1)
        load_w4(nc.sync, 2)
        load_w8(2)

        for page in pages[:-1]:
            nc.vector.memset(page[:].bitcast(I32), 0)
        nc.gpsimd.memset(pages[-1][:].bitcast(I32), 0)

        for c, cols in enumerate(CHUNKS):
            quantize_chunk(c)
            if c == 0:
                nc.vector.transpose(b_cols[:], b_rows[:])
                last_page = keep.tile([P, T], F32, name="last_page", tag="grouped_0", align_bytes=64)
                nc.vector.memset(last_page[:].bitcast(I32), 0)
                pages.append(last_page)
            else:
                before = CHUNKS[c - 1]
                y_held = keep.tile([P, HELD, width(before)], F32, name="y_held_%d" % c, tag="raw_%d_1" % c)
                for m in range(EARLY, PAGES):
                    place(m, before, y_held[:, m - EARLY])
            for m in range(EARLY):
                place(m, cols, ys[m][:, cols])
        for m in range(EARLY, PAGES):
            place(m, CHUNKS[-1], ys[m][:, CHUNKS[-1]])
        for m in range(PAGES, ROW_TILES):
            place(m, slice(0, S), ys[m][:])
